import numpy as np
import ml_dtypes


def mxq(x, axis, fmt="e4m3"):
    dtype, down = {"e4m3": (ml_dtypes.float8_e4m3fn, 7), "e5m2": (ml_dtypes.float8_e5m2, 14)}[fmt]
    v = np.moveaxis(np.asarray(x, np.float32).astype(ml_dtypes.bfloat16).astype(np.float64), axis, -1)
    blocks = v.reshape(v.shape[:-1] + (-1, 32))
    amax = np.abs(blocks).max(-1, keepdims=True)
    byte = np.maximum(np.where(amax > 0, np.frexp(amax)[1] - 1 + 127, 0) - down, 1)
    scale = np.exp2(byte - 127.0)
    codes = (blocks / scale).astype(np.float32).astype(dtype).astype(np.float64)
    return np.moveaxis((codes * scale).reshape(v.shape), -1, axis)


WIDE = False


def mx_kscale(k):
    if not WIDE:
        return np.ones(k)
    levels = np.array([10, -10, 5, -5, 0])
    if k % 512:
        return np.exp2(np.random.permutation(np.resize(levels, k // 32))).repeat(32)
    a = np.empty((k // 512, 16))
    for p in range(k // 512):
        a[p, :8] = np.random.permutation(np.resize(levels, 8))
        for g in range(8):
            far = levels[np.abs(levels - a[p, g]) >= 10]
            a[p, g + 8] = far[np.random.randint(len(far))]
    return np.exp2(a.ravel()).repeat(32)


def f64(x):
    return np.asarray(x).astype(np.float64)


def striped(idx):
    return np.tile(idx.reshape(-1, 16).T, (8, 1)).astype(np.uint16)


def unstriped(offs):
    return offs[:16].T.reshape(-1).astype(np.int64)


def striped8(idx):
    return np.concatenate([v.reshape(-1, 16).T for v in idx]).astype(np.uint16)


def unstriped8(offs):
    return np.stack([offs[16 * g:16 * g + 16].T.reshape(-1) for g in range(8)]).astype(np.int64)


E2M1 = np.array([0.0, 0.5, 1.0, 1.5, 2.0, 3.0, 4.0, 6.0, -0.0, -0.5, -1.0, -1.5, -2.0, -3.0, -4.0, -6.0])


def pack_weight(w, fmt):
    k, n = w.shape
    w = f64(np.asarray(w, np.float32).astype(ml_dtypes.bfloat16)).reshape(k // 32, 32, n)
    amax = np.abs(w).max(1)
    if fmt == "e4m3":
        byte = np.frexp(amax)[1] - 1 + 127 - 7
    else:
        mant, ex = np.frexp(amax / 6.0)
        byte = np.where(mant > 0.5, ex, ex - 1) + 127
    byte = np.clip(np.where(amax > 0, byte, 1), 1, 254)
    scaled = (w * np.exp2(127.0 - byte)[:, None, :]).reshape(k, n).astype(np.float32)
    by_word = np.ascontiguousarray(scaled.reshape(k // 512, 128, 4, n).transpose(0, 1, 3, 2))
    if fmt == "e4m3":
        words = by_word.astype(ml_dtypes.float8_e4m3fn).view(np.uint8)
    else:
        c = by_word.astype(ml_dtypes.float4_e2m1fn).view(np.uint8) & 0xF
        words = (c[..., 0::2] | (c[..., 1::2] << 4)).reshape(k // 512, 128, 2 * n)
    return np.ascontiguousarray(words), np.ascontiguousarray(byte.astype(np.uint8).reshape(k // 512, 16, n))


def unpack_weight(words, scales, fmt):
    g, _, n = scales.shape
    words = np.ascontiguousarray(words).reshape(g, 128, n, -1)
    if fmt == "e4m3":
        vals = words.view(ml_dtypes.float8_e4m3fn).astype(np.float64)
    else:
        nib = np.empty((g, 128, n, 4), np.uint8)
        nib[..., 0::2] = words & 0xF
        nib[..., 1::2] = words >> 4
        vals = E2M1[nib]
    vals = vals * np.repeat(np.exp2(scales.astype(np.float64) - 127.0), 8, axis=1)[..., None]
    return vals.transpose(0, 1, 3, 2).reshape(g * 512, n)


def pack_table(v):
    words, scales = pack_weight(v, "e4m3")
    return np.concatenate([words.reshape(words.shape[0], -1), scales.reshape(scales.shape[0], -1)], axis=1)


def unpack_table(tab):
    g, t = tab.shape[0], tab.shape[1] // 528
    return unpack_weight(tab[:, :512 * t].reshape(g, 128, t, 4), tab[:, 512 * t:].reshape(g, 16, t), "e4m3")


K, M, T, S = 1024, 1024, 512, 256


def setup_inputs():
    n = np.random.standard_normal
    s = mx_kscale(K)[:, None]
    u = mx_kscale(512)[:, None]
    p_w4 = pack_weight(n((K, M)) / np.sqrt(K) / s, "e2m1")
    return {
        "tab": pack_table(n((K, T)) * s),
        "w4_words": p_w4[0],
        "w4_scales": p_w4[1],
        "down": (n((K, 512)) / np.sqrt(K) / s * u.T).astype(np.float32),
        "up": (0.5 * n((512, M)) / np.sqrt(512) / u).astype(np.float32),
        "b": (0.3 * n(1024)).astype(np.float32),
        "wgo": np.repeat(np.random.uniform(0.5, 2.0, (8, S)), 16, axis=0).astype(np.float32),
        "offs": striped(np.random.permutation(T)[:S]),
        "offs2": striped8(np.stack([np.random.permutation(T)[:S] for _ in range(8)])),
    }


def reference(tab, w4_words, w4_scales, down, up, b, wgo, offs, offs2):
    tab_ = unpack_table(tab)[:, unstriped(offs)]
    w4_ = unpack_weight(w4_words, w4_scales, "e2m1")
    down_ = mxq(f64(down), 0, "e4m3")
    up_ = mxq(f64(up), 0, "e4m3")
    h_ = mxq(down_.T @ tab_, 0, "e4m3")
    y = w4_.T @ tab_ + up_.T @ h_
    place = unstriped8(offs2)[np.arange(M) % 128 // 16]
    out = np.zeros((M, T))
    out[np.arange(M)[:, None], place] = f64(wgo)[np.arange(M) % 128] * (y + f64(b)[:, None])
    return out

@@ -1,0 +1,217 @@
+from contextlib import ExitStack
+
+import concourse.mybir as mybir
+from concourse.masks import make_identity
+
+K, M, T, S, R = 1024, 1024, 512, 256, 512
+FLOPS = 2 * S * (K * R + K * M + R * M)
+
+F32 = mybir.dt.float32
+BF16 = mybir.dt.bfloat16
+I32 = mybir.dt.int32
+U32 = mybir.dt.uint32
+U16 = mybir.dt.uint16
+U8 = mybir.dt.uint8
+FP8X4 = mybir.dt.float8_e4m3fn_x4
+FP4X4 = mybir.dt.float4_e2m1fn_x4
+IDENT = mybir.ActivationFunctionType.Identity
+MULT = mybir.AluOpType.mult
+
+P = 128
+PACK = 4
+K_PASS = P * PACK
+PASSES = K // K_PASS
+HALF = S // 2
+ROW_TILES = M // P
+PAGES = 4
+VECTOR_COLUMNS = 88
+UP_LOADS = ((0, 2), (2, 4), (4, 8))
+W4_LOADS = ((0, 2), (2, 8))
+VECTOR_UP_TILES = 2
+SLOTS = 3
+
+
+def tile_list_tabhs_l_bias_kernel(tc, tab, w4_words, w4_scales, down, up, b, wgo, offs, offs2, out):
+    nc = tc.nc
+    with ExitStack() as ctx:
+        keep = ctx.enter_context(tc.tile_pool(name="keep", bufs=1))
+        psum = ctx.enter_context(tc.psum_pool(name="psum", bufs=1))
+
+        picks = keep.tile([P, S // 16], U16, name="picks")
+        places = keep.tile([P, S // 16], U16, name="places")
+        tab_words = keep.tile([P, PASSES, T], I32, name="tab_words", align_bytes=64)
+        tab_scales = keep.tile([P, PASSES, T], U8, name="tab_scales", align_bytes=64)
+        w4_scale = keep.tile([P, PASSES, M], U8, name="w4_scale", align_bytes=64)
+        identity = keep.tile([P, P], F32, name="identity", align_bytes=64)
+        bias_rows = keep.tile([P, P], F32, name="bias_rows", align_bytes=64)
+        bias = keep.tile([P, ROW_TILES], F32, name="bias", align_bytes=64)
+        weights = keep.tile([P, S], F32, name="weights", align_bytes=64)
+        pages = [keep.tile([P, T], F32, name=f"page{i}", align_bytes=64) for i in range(PAGES)]
+        down_raw = [keep.tile([P, PACK, R], F32, name=f"down_raw{a}", align_bytes=64) for a in range(PASSES)]
+        up_raw = [keep.tile([P, PACK, (hi - lo) * P], F32, name=f"up_raw{lo}", align_bytes=64) for lo, hi in UP_LOADS]
+        w4_codes = [keep.tile([P, PASSES, (hi - lo) * 2 * P], U8, name=f"w4_codes{lo}", align_bytes=64) for lo, hi in W4_LOADS]
+
+        def load_scale_rows(queue, plane, rows):
+            for q in range(4):
+                queue.dma_start(out=plane[32 * q : 32 * q + 4].bitcast(I32), in_=rows[4 * q : 4 * q + 4].bitcast(I32))
+
+        def load_up(u):
+            lo, hi = UP_LOADS[u]
+            nc.sync.dma_start(out=up_raw[u][:], in_=up[:, lo * P : hi * P].rearrange("(p j) n -> p j n", j=PACK))
+
+        def load_w4(u):
+            lo, hi = W4_LOADS[u]
+            nc.sync.dma_start(
+                out=w4_codes[u][:].bitcast(I32),
+                in_=w4_words[:, :, lo * 2 * P : hi * 2 * P].rearrange("a p x -> p a x").bitcast(I32),
+            )
+
+        nc.gpsimd.memset(tab_scales[:].bitcast(I32), 0)
+        nc.gpsimd.memset(bias_rows[:], 0.0)
+        nc.vector.memset(w4_scale[:].bitcast(I32), 0)
+        make_identity(nc, identity[:])
+
+        nc.sync.dma_start(out=tab_words[:], in_=tab[:, : K_PASS * T].rearrange("a (p x) -> p a x", p=P).bitcast(I32))
+        nc.sync.dma_start(picks[:], offs)
+        load_scale_rows(nc.sync, tab_scales, tab[:, K_PASS * T :].rearrange("a (q t) -> q a t", q=16))
+        nc.sync.dma_start(out=bias_rows[0:ROW_TILES, :], in_=b.rearrange("(i p) -> i p", p=P))
+        for a in range(PASSES):
+            nc.sync.dma_start(out=down_raw[a][:], in_=down[a * K_PASS : (a + 1) * K_PASS, :].rearrange("(p j) r -> p j r", j=PACK))
+        load_up(0)
+        load_scale_rows(nc.sync, w4_scale, w4_scales.rearrange("a q n -> q a n"))
+        load_w4(0)
+        nc.sync.dma_start(places[:], offs2)
+        nc.sync.dma_start(out=weights[:], in_=wgo)
+        load_up(1)
+        load_w4(1)
+        load_up(2)
+
+        for page in pages:
+            nc.vector.memset(page[:], 0.0)
+
+        bias_bank = psum.tile([P, P], F32, name="bias_bank")
+        nc.tensor.transpose(bias_bank[:], bias_rows[:], identity[:])
+        nc.scalar.activation(out=bias[:], in_=bias_bank[:, 0:ROW_TILES], func=IDENT)
+
+        v_codes, v_scales = [], []
+        for a in range(PASSES):
+            codes = keep.tile([P, S], U32, name=f"v_codes{a}", align_bytes=64)
+            scales = keep.tile([P, S], U8, name=f"v_scales{a}", align_bytes=64)
+            nc.vector.tensor_copy(codes[:], tab_words[:, a, :].bitcast(U32).indirect(picks[:]))
+            nc.vector.tensor_copy(scales[:], tab_scales[:, a, :].indirect(picks[:]))
+            v_codes.append(codes)
+            v_scales.append(scales)
+
+        h_banks = [psum.tile([P, PACK, HALF], F32, name=f"h_bank{u}", tag=f"bank{u}") for u in range(2)]
+        for a in range(PASSES):
+            grouped = keep.tile([P, PACK, P, PACK], BF16, name=f"down_grouped{a}", tag="grouped", align_bytes=64)
+            codes = keep.tile([P, PACK, P], U32, name=f"down_codes{a}", align_bytes=64)
+            scales = keep.tile([P, PACK, P], U8, name=f"down_scales{a}", align_bytes=64)
+            source = down_raw[a][:].rearrange("p j (m t) -> p m j t", t=PACK)
+            target = grouped[:].rearrange("p t m j -> p m j t")
+            nc.scalar.copy(out=target[:, VECTOR_COLUMNS:], in_=source[:, VECTOR_COLUMNS:])
+            nc.vector.tensor_copy(out=target[:, :VECTOR_COLUMNS], in_=source[:, :VECTOR_COLUMNS])
+            for t in range(PACK):
+                nc.vector.quantize_mx(
+                    out=codes[:, t, :].bitcast(FP8X4),
+                    scales=scales[:, t, :],
+                    in_=grouped[:, t].rearrange("p m j -> p (m j)"),
+                )
+            for u in range(2):
+                cols = slice(u * HALF, (u + 1) * HALF)
+                for t in range(PACK):
+                    nc.tensor.matmul_mx(
+                        out=h_banks[u][:, t, :],
+                        lhsT=codes[:, t, :].bitcast(FP8X4),
+                        lhsT_scale=scales[:, t, :],
+                        rhs=v_codes[a][:, cols].bitcast(FP8X4),
+                        rhs_scale=v_scales[a][:, cols],
+                        start=(a == 0 and t == 0),
+                        stop=(a == PASSES - 1 and t == PACK - 1),
+                    )
+
+        def up_source(i):
+            u = [lo <= i < hi for lo, hi in UP_LOADS].index(True)
+            first = (i - UP_LOADS[u][0]) * P
+            return up_raw[u][:, :, first : first + P].rearrange("p j (c e) -> p c j e", e=4)
+
+        def quantize_up(i, grouped):
+            codes = keep.tile([P, P], U32, name=f"up_codes{i}", align_bytes=64)
+            scales = keep.tile([P, P], U8, name=f"up_scales{i}", align_bytes=64)
+            nc.vector.quantize_mx(out=codes[:].bitcast(FP8X4), scales=scales[:], in_=grouped.rearrange("p n j -> p (n j)"))
+            return codes, scales
+
+        def prepare_up(i):
+            grouped = keep.tile([P, P, PACK], BF16, name=f"up_grouped{i}", tag=f"slot{i % SLOTS}", align_bytes=64)
+            nc.scalar.copy(out=grouped[:].rearrange("p (c e) j -> p c j e", e=4), in_=up_source(i))
+            return quantize_up(i, grouped[:])
+
+        def base_passes(i, bank, halves):
+            u = [lo <= i < hi for lo, hi in W4_LOADS].index(True)
+            first = (i - W4_LOADS[u][0]) * 2 * P
+            for a in range(PASSES):
+                for h in halves:
+                    cols = slice(h * HALF, (h + 1) * HALF)
+                    nc.tensor.matmul_mx(
+                        out=bank[:, cols],
+                        lhsT=w4_codes[u][:, a, first : first + 2 * P].bitcast(FP4X4),
+                        lhsT_scale=w4_scale[:, a, i * P : (i + 1) * P],
+                        rhs=v_codes[a][:, cols].bitcast(FP8X4),
+                        rhs_scale=v_scales[a][:, cols],
+                        start=(a == 0 and h == halves[0]),
+                        stop=False,
+                    )
+
+        h_codes = keep.tile([P, S], U32, name="h_codes", align_bytes=64)
+        h_scales = keep.tile([P, S], U8, name="h_scales", align_bytes=64)
+
+        def quantize_h(u):
+            grouped = keep.tile([P, HALF, PACK], BF16, name=f"h_grouped{u}", tag=f"slot{u + 1}", align_bytes=64)
+            nc.scalar.copy(out=grouped[:], in_=h_banks[u][:].rearrange("p t j -> p j t"))
+            cols = slice(u * HALF, (u + 1) * HALF)
+            nc.vector.quantize_mx(
+                out=h_codes[:, cols].bitcast(FP8X4), scales=h_scales[:, cols], in_=grouped[:].rearrange("p j t -> p (j t)")
+            )
+
+        def finish(i, bank, halves, up_q, y):
+            cols = slice(halves[0] * HALF, (halves[-1] + 1) * HALF)
+            entries = slice(cols.start // 16, cols.stop // 16)
+            nc.tensor.matmul_mx(
+                out=bank[:, cols],
+                lhsT=up_q[0][:].bitcast(FP8X4),
+                lhsT_scale=up_q[1][:],
+                rhs=h_codes[:, cols].bitcast(FP8X4),
+                rhs_scale=h_scales[:, cols],
+                start=False,
+                stop=True,
+            )
+            nc.scalar.activation(out=y[:, cols], in_=bank[:, cols], func=IDENT, bias=bias[:, i : i + 1])
+            page = pages[i % PAGES]
+            nc.vector.tensor_tensor(page[:].indirect(places[:, entries]), y[:, cols], weights[:, cols], MULT)
+
+        def store(i):
+            nc.sync.dma_start(out=out[i * P : (i + 1) * P, :], in_=pages[i % PAGES][:])
+
+        first_grouped = keep.tile(
+            [P, VECTOR_UP_TILES, P, PACK], BF16, name="first_grouped", tag="grouped", align_bytes=64
+        )
+        for i in range(VECTOR_UP_TILES):
+            nc.vector.tensor_copy(out=first_grouped[:, i].rearrange("p (c e) j -> p c j e", e=4), in_=up_source(i))
+        up_q = {0: quantize_up(0, first_grouped[:, 0])}
+        y = keep.tile([P, S], F32, name="y0", tag="slot0", align_bytes=64)
+        quantize_h(0)
+        up_q[1] = quantize_up(1, first_grouped[:, 1])
+        quantize_h(1)
+        for h in range(2):
+            bank = psum.tile([P, S], F32, name=f"y_bank0_{h}", tag=f"bank{h}")
+            base_passes(0, bank, (h,))
+            finish(0, bank, (h,), up_q[0], y)
+        store(0)
+        for i in range(1, ROW_TILES):
+            if i + 1 < ROW_TILES:
+                up_q[i + 1] = prepare_up(i + 1)
+            bank = psum.tile([P, S], F32, name=f"y_bank{i}", tag=f"bank{(i + 1) % 2}")
+            y = keep.tile([P, S], F32, name=f"y{i}", tag=f"slot{i % SLOTS}", align_bytes=64)
+            base_passes(i, bank, (0, 1))
+            finish(i, bank, (0, 1), up_q[i], y)
+            store(i)

@@ -23,12 +23,11 @@ K_PASS = P * PACK
 PASSES = K // K_PASS
 HALF = S // 2
 ROW_TILES = M // P
-PAGES = 4
-VECTOR_COLUMNS = 88
+PAGES = 3
+DOWN_LOADS = ((0, 0, 4, 88), (1, 0, 2, 88), (1, 2, 4, 88))
 UP_LOADS = ((0, 2), (2, 4), (4, 8))
 W4_LOADS = ((0, 2), (2, 8))
-VECTOR_UP_TILES = 2
-SLOTS = 3
+FIRST_UP_TILES = 3
 
 
 def tile_list_tabhs_l_bias_kernel(tc, tab, w4_words, w4_scales, down, up, b, wgo, offs, offs2, out):
@@ -39,7 +38,7 @@ def tile_list_tabhs_l_bias_kernel(tc, tab, w4_words, w4_scales, down, up, b, wgo
 
         picks = keep.tile([P, S // 16], U16, name="picks")
         places = keep.tile([P, S // 16], U16, name="places")
-        tab_words = keep.tile([P, PASSES, T], I32, name="tab_words", align_bytes=64)
+        tab_words = [keep.tile([P, T], I32, name=f"tab_words{a}", align_bytes=64) for a in range(PASSES)]
         tab_scales = keep.tile([P, PASSES, T], U8, name="tab_scales", align_bytes=64)
         w4_scale = keep.tile([P, PASSES, M], U8, name="w4_scale", align_bytes=64)
         identity = keep.tile([P, P], F32, name="identity", align_bytes=64)
@@ -47,13 +46,16 @@ def tile_list_tabhs_l_bias_kernel(tc, tab, w4_words, w4_scales, down, up, b, wgo
         bias = keep.tile([P, ROW_TILES], F32, name="bias", align_bytes=64)
         weights = keep.tile([P, S], F32, name="weights", align_bytes=64)
         pages = [keep.tile([P, T], F32, name=f"page{i}", align_bytes=64) for i in range(PAGES)]
-        down_raw = [keep.tile([P, PACK, R], F32, name=f"down_raw{a}", align_bytes=64) for a in range(PASSES)]
+        down_raw = [keep.tile([P, hi - lo, R], F32, name=f"down_raw{a}_{lo}", tag=f"down_raw{a}_{lo}", align_bytes=64) for a, lo, hi, share in DOWN_LOADS]
         up_raw = [keep.tile([P, PACK, (hi - lo) * P], F32, name=f"up_raw{lo}", align_bytes=64) for lo, hi in UP_LOADS]
         w4_codes = [keep.tile([P, PASSES, (hi - lo) * 2 * P], U8, name=f"w4_codes{lo}", align_bytes=64) for lo, hi in W4_LOADS]
 
         def load_scale_rows(queue, plane, rows):
             for q in range(4):
                 queue.dma_start(out=plane[32 * q : 32 * q + 4].bitcast(I32), in_=rows[4 * q : 4 * q + 4].bitcast(I32))
+
+        def load_tab_words(a):
+            nc.sync.dma_start(out=tab_words[a][:], in_=tab[a, : K_PASS * T].rearrange("(p x) -> p x", p=P).bitcast(I32))
 
         def load_up(u):
             lo, hi = UP_LOADS[u]
@@ -68,21 +70,23 @@ def tile_list_tabhs_l_bias_kernel(tc, tab, w4_words, w4_scales, down, up, b, wgo
 
         nc.gpsimd.memset(tab_scales[:].bitcast(I32), 0)
         nc.gpsimd.memset(bias_rows[:], 0.0)
+        nc.gpsimd.dma_start(out=bias_rows[0:ROW_TILES, :], in_=b.rearrange("(i p) -> i p", p=P))
         nc.vector.memset(w4_scale[:].bitcast(I32), 0)
         make_identity(nc, identity[:])
 
-        nc.sync.dma_start(out=tab_words[:], in_=tab[:, : K_PASS * T].rearrange("a (p x) -> p a x", p=P).bitcast(I32))
+        load_tab_words(0)
         nc.sync.dma_start(picks[:], offs)
         load_scale_rows(nc.sync, tab_scales, tab[:, K_PASS * T :].rearrange("a (q t) -> q a t", q=16))
-        nc.sync.dma_start(out=bias_rows[0:ROW_TILES, :], in_=b.rearrange("(i p) -> i p", p=P))
-        for a in range(PASSES):
-            nc.sync.dma_start(out=down_raw[a][:], in_=down[a * K_PASS : (a + 1) * K_PASS, :].rearrange("(p j) r -> p j r", j=PACK))
+        load_tab_words(1)
+        for raw, (a, lo, hi, share) in zip(down_raw, DOWN_LOADS):
+            rows = down[a * K_PASS : (a + 1) * K_PASS, :].rearrange("(p j) r -> p j r", j=PACK)
+            nc.sync.dma_start(out=raw[:], in_=rows[:, lo:hi, :])
+        nc.sync.dma_start(places[:], offs2)
         load_up(0)
+        load_up(1)
         load_scale_rows(nc.sync, w4_scale, w4_scales.rearrange("a q n -> q a n"))
         load_w4(0)
-        nc.sync.dma_start(places[:], offs2)
         nc.sync.dma_start(out=weights[:], in_=wgo)
-        load_up(1)
         load_w4(1)
         load_up(2)
 
@@ -97,7 +101,7 @@ def tile_list_tabhs_l_bias_kernel(tc, tab, w4_words, w4_scales, down, up, b, wgo
         for a in range(PASSES):
             codes = keep.tile([P, S], U32, name=f"v_codes{a}", align_bytes=64)
             scales = keep.tile([P, S], U8, name=f"v_scales{a}", align_bytes=64)
-            nc.vector.tensor_copy(codes[:], tab_words[:, a, :].bitcast(U32).indirect(picks[:]))
+            nc.vector.tensor_copy(codes[:], tab_words[a][:].bitcast(U32).indirect(picks[:]))
             nc.vector.tensor_copy(scales[:], tab_scales[:, a, :].indirect(picks[:]))
             v_codes.append(codes)
             v_scales.append(scales)
@@ -107,15 +111,18 @@ def tile_list_tabhs_l_bias_kernel(tc, tab, w4_words, w4_scales, down, up, b, wgo
             grouped = keep.tile([P, PACK, P, PACK], BF16, name=f"down_grouped{a}", tag="grouped", align_bytes=64)
             codes = keep.tile([P, PACK, P], U32, name=f"down_codes{a}", align_bytes=64)
             scales = keep.tile([P, PACK, P], U8, name=f"down_scales{a}", align_bytes=64)
-            source = down_raw[a][:].rearrange("p j (m t) -> p m j t", t=PACK)
-            target = grouped[:].rearrange("p t m j -> p m j t")
-            nc.scalar.copy(out=target[:, VECTOR_COLUMNS:], in_=source[:, VECTOR_COLUMNS:])
-            nc.vector.tensor_copy(out=target[:, :VECTOR_COLUMNS], in_=source[:, :VECTOR_COLUMNS])
-            for t in range(PACK):
+            for raw, (of_pass, lo, hi, share) in zip(down_raw, DOWN_LOADS):
+                if of_pass == a:
+                    source = raw[:].rearrange("p j (m t) -> p m j t", t=PACK)
+                    target = grouped[:, :, :, lo:hi].rearrange("p t m j -> p m j t")
+                    nc.scalar.copy(out=target[:, share:], in_=source[:, share:])
+                    nc.vector.tensor_copy(out=target[:, :share], in_=source[:, :share])
+            step = PACK // (a + 1)
+            for t in range(0, PACK, step):
                 nc.vector.quantize_mx(
-                    out=codes[:, t, :].bitcast(FP8X4),
-                    scales=scales[:, t, :],
-                    in_=grouped[:, t].rearrange("p m j -> p (m j)"),
+                    out=codes[:, t : t + step, :].rearrange("p t m -> p (t m)").bitcast(FP8X4),
+                    scales=scales[:, t : t + step, :].rearrange("p t m -> p (t m)"),
+                    in_=grouped[:, t : t + step].rearrange("p t m j -> p (t m j)"),
                 )
             for u in range(2):
                 cols = slice(u * HALF, (u + 1) * HALF)
@@ -141,10 +148,8 @@ def tile_list_tabhs_l_bias_kernel(tc, tab, w4_words, w4_scales, down, up, b, wgo
             nc.vector.quantize_mx(out=codes[:].bitcast(FP8X4), scales=scales[:], in_=grouped.rearrange("p n j -> p (n j)"))
             return codes, scales
 
-        def prepare_up(i):
-            grouped = keep.tile([P, P, PACK], BF16, name=f"up_grouped{i}", tag=f"slot{i % SLOTS}", align_bytes=64)
-            nc.scalar.copy(out=grouped[:].rearrange("p (c e) j -> p c j e", e=4), in_=up_source(i))
-            return quantize_up(i, grouped[:])
+        def group_up(copy, i, grouped):
+            copy(out=grouped.rearrange("p (c e) j -> p c j e", e=4), in_=up_source(i))
 
         def base_passes(i, bank, halves):
             u = [lo <= i < hi for lo, hi in W4_LOADS].index(True)
@@ -166,7 +171,7 @@ def tile_list_tabhs_l_bias_kernel(tc, tab, w4_words, w4_scales, down, up, b, wgo
         h_scales = keep.tile([P, S], U8, name="h_scales", align_bytes=64)
 
         def quantize_h(u):
-            grouped = keep.tile([P, HALF, PACK], BF16, name=f"h_grouped{u}", tag=f"slot{u + 1}", align_bytes=64)
+            grouped = keep.tile([P, HALF, PACK], BF16, name=f"h_grouped{u}", tag=f"h_grouped{u}", align_bytes=64)
             nc.scalar.copy(out=grouped[:], in_=h_banks[u][:].rearrange("p t j -> p j t"))
             cols = slice(u * HALF, (u + 1) * HALF)
             nc.vector.quantize_mx(
@@ -192,26 +197,24 @@ def tile_list_tabhs_l_bias_kernel(tc, tab, w4_words, w4_scales, down, up, b, wgo
         def store(i):
             nc.sync.dma_start(out=out[i * P : (i + 1) * P, :], in_=pages[i % PAGES][:])
 
-        first_grouped = keep.tile(
-            [P, VECTOR_UP_TILES, P, PACK], BF16, name="first_grouped", tag="grouped", align_bytes=64
-        )
-        for i in range(VECTOR_UP_TILES):
-            nc.vector.tensor_copy(out=first_grouped[:, i].rearrange("p (c e) j -> p c j e", e=4), in_=up_source(i))
-        up_q = {0: quantize_up(0, first_grouped[:, 0])}
-        y = keep.tile([P, S], F32, name="y0", tag="slot0", align_bytes=64)
+        by_scalar = keep.tile([P, P, PACK], BF16, name="by_scalar", tag="down_raw1_2", align_bytes=64)
+        by_vector = keep.tile([P, 2, P, PACK], BF16, name="by_vector", tag="grouped", align_bytes=64)
+        group_up(nc.scalar.copy, 1, by_scalar[:])
+        group_up(nc.vector.tensor_copy, 0, by_vector[:, 0])
+        up_q = {1: quantize_up(1, by_scalar[:])}
+        up_q[0] = quantize_up(0, by_vector[:, 0])
         quantize_h(0)
-        up_q[1] = quantize_up(1, first_grouped[:, 1])
+        group_up(nc.vector.tensor_copy, 2, by_vector[:, 1])
         quantize_h(1)
-        for h in range(2):
-            bank = psum.tile([P, S], F32, name=f"y_bank0_{h}", tag=f"bank{h}")
-            base_passes(0, bank, (h,))
-            finish(0, bank, (h,), up_q[0], y)
-        store(0)
-        for i in range(1, ROW_TILES):
-            if i + 1 < ROW_TILES:
-                up_q[i + 1] = prepare_up(i + 1)
-            bank = psum.tile([P, S], F32, name=f"y_bank{i}", tag=f"bank{(i + 1) % 2}")
-            y = keep.tile([P, S], F32, name=f"y{i}", tag=f"slot{i % SLOTS}", align_bytes=64)
-            base_passes(i, bank, (0, 1))
-            finish(i, bank, (0, 1), up_q[i], y)
+        up_q[2] = quantize_up(2, by_vector[:, 1])
+        for i in range(ROW_TILES):
+            work = keep.tile([P, 2, S], F32, name=f"work{i}", tag=f"work{i % 2}", align_bytes=64)
+            if FIRST_UP_TILES <= i + 1 < ROW_TILES:
+                grouped = work[:, 1, :].bitcast(BF16).rearrange("p (n j) -> p n j", j=PACK)
+                group_up(nc.scalar.copy, i + 1, grouped)
+                up_q[i + 1] = quantize_up(i + 1, grouped)
+            for halves in ((0,), (1,)) if i == 0 else ((0, 1),):
+                bank = psum.tile([P, S], F32, name=f"y_bank{i}_{halves[0]}", tag=f"bank{(i + halves[-1]) % 2}")
+                base_passes(i, bank, halves)
+                finish(i, bank, halves, up_q[i], work[:, 0, :])
             store(i)

@@ -23,9 +23,10 @@ K_PASS = P * PACK
 PASSES = K // K_PASS
 HALF = S // 2
 ROW_TILES = M // P
-PAGES = 3
+PAGES = 4
+Y_TILES = 3
 DOWN_LOADS = ((0, 0, 4, 88), (1, 0, 2, 88), (1, 2, 4, 88))
-UP_LOADS = ((0, 2), (2, 4), (4, 8))
+UP_LOADS = ((0, 2), (2, 3), (3, 5), (5, 8))
 W4_LOADS = ((0, 2), (2, 8))
 FIRST_UP_TILES = 3
 
@@ -83,12 +84,13 @@ def tile_list_tabhs_l_bias_kernel(tc, tab, w4_words, w4_scales, down, up, b, wgo
             nc.sync.dma_start(out=raw[:], in_=rows[:, lo:hi, :])
         nc.sync.dma_start(places[:], offs2)
         load_up(0)
-        load_up(1)
         load_scale_rows(nc.sync, w4_scale, w4_scales.rearrange("a q n -> q a n"))
         load_w4(0)
+        load_up(1)
         nc.sync.dma_start(out=weights[:], in_=wgo)
-        load_w4(1)
         load_up(2)
+        load_w4(1)
+        load_up(3)
 
         for page in pages:
             nc.vector.memset(page[:], 0.0)
@@ -143,7 +145,7 @@ def tile_list_tabhs_l_bias_kernel(tc, tab, w4_words, w4_scales, down, up, b, wgo
             return up_raw[u][:, :, first : first + P].rearrange("p j (c e) -> p c j e", e=4)
 
         def quantize_up(i, grouped):
-            codes = keep.tile([P, P], U32, name=f"up_codes{i}", align_bytes=64)
+            codes = keep.tile([P, P], U32, name=f"up_codes{i}", tag=f"up{i}", align_bytes=64)
             scales = keep.tile([P, P], U8, name=f"up_scales{i}", align_bytes=64)
             nc.vector.quantize_mx(out=codes[:].bitcast(FP8X4), scales=scales[:], in_=grouped.rearrange("p n j -> p (n j)"))
             return codes, scales
@@ -208,13 +210,13 @@ def tile_list_tabhs_l_bias_kernel(tc, tab, w4_words, w4_scales, down, up, b, wgo
         quantize_h(1)
         up_q[2] = quantize_up(2, by_vector[:, 1])
         for i in range(ROW_TILES):
-            work = keep.tile([P, 2, S], F32, name=f"work{i}", tag=f"work{i % 2}", align_bytes=64)
+            y = keep.tile([P, S], F32, name=f"y{i}", tag=f"y{i % Y_TILES}", align_bytes=64)
             if FIRST_UP_TILES <= i + 1 < ROW_TILES:
-                grouped = work[:, 1, :].bitcast(BF16).rearrange("p (n j) -> p n j", j=PACK)
-                group_up(nc.scalar.copy, i + 1, grouped)
-                up_q[i + 1] = quantize_up(i + 1, grouped)
+                grouped = keep.tile([P, P, PACK], BF16, name=f"up_grouped{i + 1}", tag=f"up{i - 1}", align_bytes=64)
+                group_up(nc.scalar.copy, i + 1, grouped[:])
+                up_q[i + 1] = quantize_up(i + 1, grouped[:])
             for halves in ((0,), (1,)) if i == 0 else ((0, 1),):
                 bank = psum.tile([P, S], F32, name=f"y_bank{i}_{halves[0]}", tag=f"bank{(i + halves[-1]) % 2}")
                 base_passes(i, bank, halves)
-                finish(i, bank, halves, up_q[i], work[:, 0, :])
+                finish(i, bank, halves, up_q[i], y)
             store(i)

@@ -28,7 +28,7 @@ Y_TILES = 3
 DOWN_LOADS = ((0, 0, 4, 88), (1, 0, 2, 88), (1, 2, 4, 88))
 UP_LOADS = ((0, 2), (2, 3), (3, 5), (5, 8))
 W4_LOADS = ((0, 2), (2, 8))
-FIRST_UP_TILES = 3
+FIRST_UP_TILES = 2
 
 
 def tile_list_tabhs_l_bias_kernel(tc, tab, w4_words, w4_scales, down, up, b, wgo, offs, offs2, out):
@@ -47,7 +47,7 @@ def tile_list_tabhs_l_bias_kernel(tc, tab, w4_words, w4_scales, down, up, b, wgo
         bias = keep.tile([P, ROW_TILES], F32, name="bias", align_bytes=64)
         weights = keep.tile([P, S], F32, name="weights", align_bytes=64)
         pages = [keep.tile([P, T], F32, name=f"page{i}", align_bytes=64) for i in range(PAGES)]
-        down_raw = [keep.tile([P, hi - lo, R], F32, name=f"down_raw{a}_{lo}", tag=f"down_raw{a}_{lo}", align_bytes=64) for a, lo, hi, share in DOWN_LOADS]
+        down_raw = [keep.tile([P, hi - lo, R], F32, name=f"down_raw{a}_{lo}", align_bytes=64) for a, lo, hi, share in DOWN_LOADS]
         up_raw = [keep.tile([P, PACK, (hi - lo) * P], F32, name=f"up_raw{lo}", align_bytes=64) for lo, hi in UP_LOADS]
         w4_codes = [keep.tile([P, PASSES, (hi - lo) * 2 * P], U8, name=f"w4_codes{lo}", align_bytes=64) for lo, hi in W4_LOADS]
 
@@ -86,8 +86,8 @@ def tile_list_tabhs_l_bias_kernel(tc, tab, w4_words, w4_scales, down, up, b, wgo
         load_up(0)
         load_scale_rows(nc.sync, w4_scale, w4_scales.rearrange("a q n -> q a n"))
         load_w4(0)
-        load_up(1)
         nc.sync.dma_start(out=weights[:], in_=wgo)
+        load_up(1)
         load_up(2)
         load_w4(1)
         load_up(3)
@@ -199,16 +199,13 @@ def tile_list_tabhs_l_bias_kernel(tc, tab, w4_words, w4_scales, down, up, b, wgo
         def store(i):
             nc.sync.dma_start(out=out[i * P : (i + 1) * P, :], in_=pages[i % PAGES][:])
 
-        by_scalar = keep.tile([P, P, PACK], BF16, name="by_scalar", tag="down_raw1_2", align_bytes=64)
-        by_vector = keep.tile([P, 2, P, PACK], BF16, name="by_vector", tag="grouped", align_bytes=64)
-        group_up(nc.scalar.copy, 1, by_scalar[:])
-        group_up(nc.vector.tensor_copy, 0, by_vector[:, 0])
-        up_q = {1: quantize_up(1, by_scalar[:])}
-        up_q[0] = quantize_up(0, by_vector[:, 0])
+        first_grouped = keep.tile([P, FIRST_UP_TILES, P, PACK], BF16, name="first_grouped", tag="grouped", align_bytes=64)
+        for i in range(FIRST_UP_TILES):
+            group_up(nc.vector.tensor_copy, i, first_grouped[:, i])
+        up_q = {0: quantize_up(0, first_grouped[:, 0])}
         quantize_h(0)
-        group_up(nc.vector.tensor_copy, 2, by_vector[:, 1])
+        up_q[1] = quantize_up(1, first_grouped[:, 1])
         quantize_h(1)
-        up_q[2] = quantize_up(2, by_vector[:, 1])
         for i in range(ROW_TILES):
             y = keep.tile([P, S], F32, name=f"y{i}", tag=f"y{i % Y_TILES}", align_bytes=64)
             if FIRST_UP_TILES <= i + 1 < ROW_TILES:

@@ -21,11 +21,16 @@ P = 128
 PACK = 4
 K_PASS = P * PACK
 PASSES = K // K_PASS
+BLOCKS = K_PASS // 32
+QUADRANTS = 4
+LIST_ROWS = 16
+LINE = 4
 HALF = S // 2
 ROW_TILES = M // P
 PAGES = 4
 Y_TILES = 3
-DOWN_LOADS = ((0, 0, 4, 88), (1, 0, 2, 88), (1, 2, 4, 88))
+VECTOR_PLACES = 88
+DOWN_LOADS = ((0, 0, 4), (1, 0, 2), (1, 2, 4))
 UP_LOADS = ((0, 2), (2, 3), (3, 5), (5, 8))
 W4_LOADS = ((0, 2), (2, 8))
 FIRST_UP_TILES = 2
@@ -37,8 +42,8 @@ def tile_list_tabhs_l_bias_kernel(tc, tab, w4_words, w4_scales, down, up, b, wgo
         keep = ctx.enter_context(tc.tile_pool(name="keep", bufs=1))
         psum = ctx.enter_context(tc.psum_pool(name="psum", bufs=1))
 
-        picks = keep.tile([P, S // 16], U16, name="picks")
-        places = keep.tile([P, S // 16], U16, name="places")
+        picks = keep.tile([P, S // LIST_ROWS], U16, name="picks")
+        places = keep.tile([P, S // LIST_ROWS], U16, name="places")
         tab_words = [keep.tile([P, T], I32, name=f"tab_words{a}", align_bytes=64) for a in range(PASSES)]
         tab_scales = keep.tile([P, PASSES, T], U8, name="tab_scales", align_bytes=64)
         w4_scale = keep.tile([P, PASSES, M], U8, name="w4_scale", align_bytes=64)
@@ -47,20 +52,30 @@ def tile_list_tabhs_l_bias_kernel(tc, tab, w4_words, w4_scales, down, up, b, wgo
         bias = keep.tile([P, ROW_TILES], F32, name="bias", align_bytes=64)
         weights = keep.tile([P, S], F32, name="weights", align_bytes=64)
         pages = [keep.tile([P, T], F32, name=f"page{i}", align_bytes=64) for i in range(PAGES)]
-        down_raw = [keep.tile([P, hi - lo, R], F32, name=f"down_raw{a}_{lo}", align_bytes=64) for a, lo, hi, share in DOWN_LOADS]
+        down_raw = [
+            keep.tile([P, hi - lo, R], F32, name=f"down_raw{n}", tag=f"down_raw{n}", align_bytes=64)
+            for n, (a, lo, hi) in enumerate(DOWN_LOADS)
+        ]
         up_raw = [keep.tile([P, PACK, (hi - lo) * P], F32, name=f"up_raw{lo}", align_bytes=64) for lo, hi in UP_LOADS]
         w4_codes = [keep.tile([P, PASSES, (hi - lo) * 2 * P], U8, name=f"w4_codes{lo}", align_bytes=64) for lo, hi in W4_LOADS]
 
-        def load_scale_rows(queue, plane, rows):
-            for q in range(4):
-                queue.dma_start(out=plane[32 * q : 32 * q + 4].bitcast(I32), in_=rows[4 * q : 4 * q + 4].bitcast(I32))
+        def half_columns(u):
+            return slice(u * HALF, (u + 1) * HALF)
+
+        def list_columns(cols):
+            return slice(cols.start // LIST_ROWS, cols.stop // LIST_ROWS)
+
+        def load_scale_rows(scale_tile, rows):
+            n = BLOCKS // QUADRANTS
+            for Q in range(QUADRANTS):
+                nc.sync.dma_start(out=scale_tile[32 * Q : 32 * Q + n].bitcast(I32), in_=rows[n * Q : n * Q + n].bitcast(I32))
 
         def load_tab_words(a):
             nc.sync.dma_start(out=tab_words[a][:], in_=tab[a, : K_PASS * T].rearrange("(p x) -> p x", p=P).bitcast(I32))
 
         def load_up(u):
             lo, hi = UP_LOADS[u]
-            nc.sync.dma_start(out=up_raw[u][:], in_=up[:, lo * P : hi * P].rearrange("(p j) n -> p j n", j=PACK))
+            nc.sync.dma_start(out=up_raw[u][:], in_=up[:, lo * P : hi * P].rearrange("(p i) n -> p i n", i=PACK))
 
         def load_w4(u):
             lo, hi = W4_LOADS[u]
@@ -77,14 +92,14 @@ def tile_list_tabhs_l_bias_kernel(tc, tab, w4_words, w4_scales, down, up, b, wgo
 
         load_tab_words(0)
         nc.sync.dma_start(picks[:], offs)
-        load_scale_rows(nc.sync, tab_scales, tab[:, K_PASS * T :].rearrange("a (q t) -> q a t", q=16))
-        load_tab_words(1)
-        for raw, (a, lo, hi, share) in zip(down_raw, DOWN_LOADS):
-            rows = down[a * K_PASS : (a + 1) * K_PASS, :].rearrange("(p j) r -> p j r", j=PACK)
+        load_scale_rows(tab_scales, tab[:, K_PASS * T :].rearrange("a (q t) -> q a t", q=BLOCKS))
+        for raw, (a, lo, hi) in zip(down_raw, DOWN_LOADS):
+            rows = down[a * K_PASS : (a + 1) * K_PASS, :].rearrange("(p i) r -> p i r", i=PACK)
             nc.sync.dma_start(out=raw[:], in_=rows[:, lo:hi, :])
+        load_tab_words(1)
         nc.sync.dma_start(places[:], offs2)
         load_up(0)
-        load_scale_rows(nc.sync, w4_scale, w4_scales.rearrange("a q n -> q a n"))
+        load_scale_rows(w4_scale, w4_scales.rearrange("a q n -> q a n"))
         load_w4(0)
         nc.sync.dma_start(out=weights[:], in_=wgo)
         load_up(1)
@@ -99,66 +114,94 @@ def tile_list_tabhs_l_bias_kernel(tc, tab, w4_words, w4_scales, down, up, b, wgo
         nc.tensor.transpose(bias_bank[:], bias_rows[:], identity[:])
         nc.scalar.activation(out=bias[:], in_=bias_bank[:, 0:ROW_TILES], func=IDENT)
 
-        v_codes, v_scales = [], []
+        v_codes = [
+            keep.tile([P, S], U32, name="v_codes0", align_bytes=64),
+            keep.tile([P, S], U32, name="v_codes1", tag=f"down_raw{len(DOWN_LOADS) - 1}", align_bytes=64),
+        ]
+        v_scales = [keep.tile([P, S], U8, name=f"v_scales{a}", align_bytes=64) for a in range(PASSES)]
+
+        def gather_words(a, cols):
+            nc.vector.tensor_copy(v_codes[a][:, cols], tab_words[a][:].bitcast(U32).indirect(picks[:, list_columns(cols)]))
+
+        gather_words(0, slice(0, S))
         for a in range(PASSES):
-            codes = keep.tile([P, S], U32, name=f"v_codes{a}", align_bytes=64)
-            scales = keep.tile([P, S], U8, name=f"v_scales{a}", align_bytes=64)
-            nc.vector.tensor_copy(codes[:], tab_words[a][:].bitcast(U32).indirect(picks[:]))
-            nc.vector.tensor_copy(scales[:], tab_scales[:, a, :].indirect(picks[:]))
-            v_codes.append(codes)
-            v_scales.append(scales)
+            nc.vector.tensor_copy(v_scales[a][:], tab_scales[:, a, :].indirect(picks[:]))
 
         h_banks = [psum.tile([P, PACK, HALF], F32, name=f"h_bank{u}", tag=f"bank{u}") for u in range(2)]
-        for a in range(PASSES):
+
+        def group_down(a):
             grouped = keep.tile([P, PACK, P, PACK], BF16, name=f"down_grouped{a}", tag="grouped", align_bytes=64)
+            for raw, (of_pass, lo, hi) in zip(down_raw, DOWN_LOADS):
+                if of_pass == a:
+                    source = raw[:].rearrange("p i (m t) -> p m i t", t=PACK)
+                    target = grouped[:, :, :, lo:hi].rearrange("p t m i -> p m i t")
+                    nc.scalar.copy(out=target[:, VECTOR_PLACES:], in_=source[:, VECTOR_PLACES:])
+                    nc.vector.tensor_copy(out=target[:, :VECTOR_PLACES], in_=source[:, :VECTOR_PLACES])
+            return grouped
+
+        def quantize_down(a, grouped, slices):
             codes = keep.tile([P, PACK, P], U32, name=f"down_codes{a}", align_bytes=64)
             scales = keep.tile([P, PACK, P], U8, name=f"down_scales{a}", align_bytes=64)
-            for raw, (of_pass, lo, hi, share) in zip(down_raw, DOWN_LOADS):
-                if of_pass == a:
-                    source = raw[:].rearrange("p j (m t) -> p m j t", t=PACK)
-                    target = grouped[:, :, :, lo:hi].rearrange("p t m j -> p m j t")
-                    nc.scalar.copy(out=target[:, share:], in_=source[:, share:])
-                    nc.vector.tensor_copy(out=target[:, :share], in_=source[:, :share])
-            step = PACK // (a + 1)
-            for t in range(0, PACK, step):
+            for t in range(0, PACK, slices):
                 nc.vector.quantize_mx(
-                    out=codes[:, t : t + step, :].rearrange("p t m -> p (t m)").bitcast(FP8X4),
-                    scales=scales[:, t : t + step, :].rearrange("p t m -> p (t m)"),
-                    in_=grouped[:, t : t + step].rearrange("p t m j -> p (t m j)"),
+                    out=codes[:, t : t + slices, :].rearrange("p t m -> p (t m)").bitcast(FP8X4),
+                    scales=scales[:, t : t + slices, :].rearrange("p t m -> p (t m)"),
+                    in_=grouped[:, t : t + slices].rearrange("p t m i -> p (t m i)"),
                 )
-            for u in range(2):
-                cols = slice(u * HALF, (u + 1) * HALF)
-                for t in range(PACK):
-                    nc.tensor.matmul_mx(
-                        out=h_banks[u][:, t, :],
-                        lhsT=codes[:, t, :].bitcast(FP8X4),
-                        lhsT_scale=scales[:, t, :],
-                        rhs=v_codes[a][:, cols].bitcast(FP8X4),
-                        rhs_scale=v_scales[a][:, cols],
-                        start=(a == 0 and t == 0),
-                        stop=(a == PASSES - 1 and t == PACK - 1),
-                    )
+            return codes, scales
 
-        def up_source(i):
+        def h_passes(a, u, down_q):
+            cols = half_columns(u)
+            for t in range(PACK):
+                nc.tensor.matmul_mx(
+                    out=h_banks[u][:, t, :],
+                    lhsT=down_q[0][:, t, :].bitcast(FP8X4),
+                    lhsT_scale=down_q[1][:, t, :],
+                    rhs=v_codes[a][:, cols].bitcast(FP8X4),
+                    rhs_scale=v_scales[a][:, cols],
+                    start=(a == 0 and t == 0),
+                    stop=(a == PASSES - 1 and t == PACK - 1),
+                )
+
+        down_q = quantize_down(0, group_down(0), PACK)
+        for u in range(2):
+            h_passes(0, u, down_q)
+        last_grouped = group_down(1)
+        gather_words(1, half_columns(0))
+        down_q = quantize_down(1, last_grouped, PACK // 2)
+        gather_words(1, half_columns(1))
+        for u in range(2):
+            h_passes(1, u, down_q)
+
+        def group_up(copy, i, grouped):
             u = [lo <= i < hi for lo, hi in UP_LOADS].index(True)
             first = (i - UP_LOADS[u][0]) * P
-            return up_raw[u][:, :, first : first + P].rearrange("p j (c e) -> p c j e", e=4)
+            source = up_raw[u][:, :, first : first + P].rearrange("p e (c n) -> p c e n", n=LINE)
+            copy(out=grouped.rearrange("p (c n) e -> p c e n", n=LINE), in_=source)
 
         def quantize_up(i, grouped):
             codes = keep.tile([P, P], U32, name=f"up_codes{i}", tag=f"up{i}", align_bytes=64)
             scales = keep.tile([P, P], U8, name=f"up_scales{i}", align_bytes=64)
-            nc.vector.quantize_mx(out=codes[:].bitcast(FP8X4), scales=scales[:], in_=grouped.rearrange("p n j -> p (n j)"))
+            nc.vector.quantize_mx(out=codes[:].bitcast(FP8X4), scales=scales[:], in_=grouped.rearrange("p n e -> p (n e)"))
             return codes, scales
 
-        def group_up(copy, i, grouped):
-            copy(out=grouped.rearrange("p (c e) j -> p c j e", e=4), in_=up_source(i))
+        h_codes = keep.tile([P, S], U32, name="h_codes", align_bytes=64)
+        h_scales = keep.tile([P, S], U8, name="h_scales", align_bytes=64)
 
-        def base_passes(i, bank, halves):
+        def quantize_h(u):
+            grouped = keep.tile([P, HALF, PACK], BF16, name=f"h_grouped{u}", align_bytes=64)
+            nc.scalar.copy(out=grouped[:], in_=h_banks[u][:].rearrange("p t j -> p j t"))
+            cols = half_columns(u)
+            nc.vector.quantize_mx(
+                out=h_codes[:, cols].bitcast(FP8X4), scales=h_scales[:, cols], in_=grouped[:].rearrange("p j t -> p (j t)")
+            )
+
+        def open_sum(i, bank, halves):
             u = [lo <= i < hi for lo, hi in W4_LOADS].index(True)
             first = (i - W4_LOADS[u][0]) * 2 * P
             for a in range(PASSES):
                 for h in halves:
-                    cols = slice(h * HALF, (h + 1) * HALF)
+                    cols = half_columns(h)
                     nc.tensor.matmul_mx(
                         out=bank[:, cols],
                         lhsT=w4_codes[u][:, a, first : first + 2 * P].bitcast(FP4X4),
@@ -169,24 +212,12 @@ def tile_list_tabhs_l_bias_kernel(tc, tab, w4_words, w4_scales, down, up, b, wgo
                         stop=False,
                     )
 
-        h_codes = keep.tile([P, S], U32, name="h_codes", align_bytes=64)
-        h_scales = keep.tile([P, S], U8, name="h_scales", align_bytes=64)
-
-        def quantize_h(u):
-            grouped = keep.tile([P, HALF, PACK], BF16, name=f"h_grouped{u}", tag=f"h_grouped{u}", align_bytes=64)
-            nc.scalar.copy(out=grouped[:], in_=h_banks[u][:].rearrange("p t j -> p j t"))
-            cols = slice(u * HALF, (u + 1) * HALF)
-            nc.vector.quantize_mx(
-                out=h_codes[:, cols].bitcast(FP8X4), scales=h_scales[:, cols], in_=grouped[:].rearrange("p j t -> p (j t)")
-            )
-
-        def finish(i, bank, halves, up_q, y):
+        def close_and_scatter(i, bank, halves, up_tile, y):
             cols = slice(halves[0] * HALF, (halves[-1] + 1) * HALF)
-            entries = slice(cols.start // 16, cols.stop // 16)
             nc.tensor.matmul_mx(
                 out=bank[:, cols],
-                lhsT=up_q[0][:].bitcast(FP8X4),
-                lhsT_scale=up_q[1][:],
+                lhsT=up_tile[0][:].bitcast(FP8X4),
+                lhsT_scale=up_tile[1][:],
                 rhs=h_codes[:, cols].bitcast(FP8X4),
                 rhs_scale=h_scales[:, cols],
                 start=False,
@@ -194,10 +225,7 @@ def tile_list_tabhs_l_bias_kernel(tc, tab, w4_words, w4_scales, down, up, b, wgo
             )
             nc.scalar.activation(out=y[:, cols], in_=bank[:, cols], func=IDENT, bias=bias[:, i : i + 1])
             page = pages[i % PAGES]
-            nc.vector.tensor_tensor(page[:].indirect(places[:, entries]), y[:, cols], weights[:, cols], MULT)
-
-        def store(i):
-            nc.sync.dma_start(out=out[i * P : (i + 1) * P, :], in_=pages[i % PAGES][:])
+            nc.vector.tensor_tensor(page[:].indirect(places[:, list_columns(cols)]), y[:, cols], weights[:, cols], MULT)
 
         first_grouped = keep.tile([P, FIRST_UP_TILES, P, PACK], BF16, name="first_grouped", tag="grouped", align_bytes=64)
         for i in range(FIRST_UP_TILES):
@@ -206,14 +234,15 @@ def tile_list_tabhs_l_bias_kernel(tc, tab, w4_words, w4_scales, down, up, b, wgo
         quantize_h(0)
         up_q[1] = quantize_up(1, first_grouped[:, 1])
         quantize_h(1)
+
         for i in range(ROW_TILES):
             y = keep.tile([P, S], F32, name=f"y{i}", tag=f"y{i % Y_TILES}", align_bytes=64)
             if FIRST_UP_TILES <= i + 1 < ROW_TILES:
-                grouped = keep.tile([P, P, PACK], BF16, name=f"up_grouped{i + 1}", tag=f"up{i - 1}", align_bytes=64)
-                group_up(nc.scalar.copy, i + 1, grouped[:])
-                up_q[i + 1] = quantize_up(i + 1, grouped[:])
+                next_grouped = keep.tile([P, P, PACK], BF16, name=f"up_grouped{i + 1}", tag=f"up{i - 1}", align_bytes=64)
+                group_up(nc.scalar.copy, i + 1, next_grouped[:])
+                up_q[i + 1] = quantize_up(i + 1, next_grouped[:])
             for halves in ((0,), (1,)) if i == 0 else ((0, 1),):
                 bank = psum.tile([P, S], F32, name=f"y_bank{i}_{halves[0]}", tag=f"bank{(i + halves[-1]) % 2}")
-                base_passes(i, bank, halves)
-                finish(i, bank, halves, up_q[i], y)
-            store(i)
+                open_sum(i, bank, halves)
+                close_and_scatter(i, bank, halves, up_q[i], y)
+            nc.sync.dma_start(out=out[i * P : (i + 1) * P, :], in_=pages[i % PAGES][:])

from contextlib import ExitStack

import concourse.mybir as mybir
from concourse.masks import make_identity

K, M, T, S, R = 1024, 1024, 512, 256, 512
FLOPS = 2 * S * (K * R + K * M + R * M)

F32 = mybir.dt.float32
BF16 = mybir.dt.bfloat16
I32 = mybir.dt.int32
U32 = mybir.dt.uint32
U16 = mybir.dt.uint16
U8 = mybir.dt.uint8
FP8X4 = mybir.dt.float8_e4m3fn_x4
FP4X4 = mybir.dt.float4_e2m1fn_x4
IDENT = mybir.ActivationFunctionType.Identity
MULT = mybir.AluOpType.mult

P = 128
PACK = 4
K_PASS = P * PACK
PASSES = K // K_PASS
BLOCKS = K_PASS // 32
QUADRANTS = 4
LIST_ROWS = 16
LINE = 4
HALF = S // 2
ROW_TILES = M // P
PAGES = 4
Y_TILES = 3
VECTOR_PLACES = 88
DOWN_LOADS = ((0, 0, 4), (1, 0, 2), (1, 2, 4))
UP_LOADS = ((0, 2), (2, 3), (3, 5), (5, 8))
W4_LOADS = ((0, 2), (2, 8))
FIRST_UP_TILES = 2


def tile_list_tabhs_l_bias_kernel(tc, tab, w4_words, w4_scales, down, up, b, wgo, offs, offs2, out):
    nc = tc.nc
    with ExitStack() as ctx:
        keep = ctx.enter_context(tc.tile_pool(name="keep", bufs=1))
        psum = ctx.enter_context(tc.psum_pool(name="psum", bufs=1))

        picks = keep.tile([P, S // LIST_ROWS], U16, name="picks")
        places = keep.tile([P, S // LIST_ROWS], U16, name="places")
        tab_words = [keep.tile([P, T], I32, name=f"tab_words{a}", align_bytes=64) for a in range(PASSES)]
        tab_scales = keep.tile([P, PASSES, T], U8, name="tab_scales", align_bytes=64)
        w4_scale = keep.tile([P, PASSES, M], U8, name="w4_scale", align_bytes=64)
        identity = keep.tile([P, P], F32, name="identity", align_bytes=64)
        bias_rows = keep.tile([P, P], F32, name="bias_rows", align_bytes=64)
        bias = keep.tile([P, ROW_TILES], F32, name="bias", align_bytes=64)
        weights = keep.tile([P, S], F32, name="weights", align_bytes=64)
        pages = [keep.tile([P, T], F32, name=f"page{i}", align_bytes=64) for i in range(PAGES)]
        down_raw = [
            keep.tile([P, hi - lo, R], F32, name=f"down_raw{n}", tag=f"down_raw{n}", align_bytes=64)
            for n, (a, lo, hi) in enumerate(DOWN_LOADS)
        ]
        up_raw = [keep.tile([P, PACK, (hi - lo) * P], F32, name=f"up_raw{lo}", align_bytes=64) for lo, hi in UP_LOADS]
        w4_codes = [keep.tile([P, PASSES, (hi - lo) * 2 * P], U8, name=f"w4_codes{lo}", align_bytes=64) for lo, hi in W4_LOADS]

        def half_columns(u):
            return slice(u * HALF, (u + 1) * HALF)

        def list_columns(cols):
            return slice(cols.start // LIST_ROWS, cols.stop // LIST_ROWS)

        def load_scale_rows(scale_tile, rows):
            n = BLOCKS // QUADRANTS
            for Q in range(QUADRANTS):
                nc.sync.dma_start(out=scale_tile[32 * Q : 32 * Q + n].bitcast(I32), in_=rows[n * Q : n * Q + n].bitcast(I32))

        def load_tab_words(a):
            nc.sync.dma_start(out=tab_words[a][:], in_=tab[a, : K_PASS * T].rearrange("(p x) -> p x", p=P).bitcast(I32))

        def load_up(u):
            lo, hi = UP_LOADS[u]
            nc.sync.dma_start(out=up_raw[u][:], in_=up[:, lo * P : hi * P].rearrange("(p i) n -> p i n", i=PACK))

        def load_w4(u):
            lo, hi = W4_LOADS[u]
            nc.sync.dma_start(
                out=w4_codes[u][:].bitcast(I32),
                in_=w4_words[:, :, lo * 2 * P : hi * 2 * P].rearrange("a p x -> p a x").bitcast(I32),
            )

        nc.gpsimd.memset(tab_scales[:].bitcast(I32), 0)
        nc.gpsimd.memset(bias_rows[:], 0.0)
        nc.gpsimd.dma_start(out=bias_rows[0:ROW_TILES, :], in_=b.rearrange("(i p) -> i p", p=P))
        nc.vector.memset(w4_scale[:].bitcast(I32), 0)
        make_identity(nc, identity[:])

        load_tab_words(0)
        nc.sync.dma_start(picks[:], offs)
        load_scale_rows(tab_scales, tab[:, K_PASS * T :].rearrange("a (q t) -> q a t", q=BLOCKS))
        for raw, (a, lo, hi) in zip(down_raw, DOWN_LOADS):
            rows = down[a * K_PASS : (a + 1) * K_PASS, :].rearrange("(p i) r -> p i r", i=PACK)
            nc.sync.dma_start(out=raw[:], in_=rows[:, lo:hi, :])
        load_tab_words(1)
        nc.sync.dma_start(places[:], offs2)
        load_up(0)
        load_scale_rows(w4_scale, w4_scales.rearrange("a q n -> q a n"))
        load_w4(0)
        nc.sync.dma_start(out=weights[:], in_=wgo)
        load_up(1)
        load_up(2)
        load_w4(1)
        load_up(3)

        for page in pages:
            nc.vector.memset(page[:], 0.0)

        bias_bank = psum.tile([P, P], F32, name="bias_bank")
        nc.tensor.transpose(bias_bank[:], bias_rows[:], identity[:])
        nc.scalar.activation(out=bias[:], in_=bias_bank[:, 0:ROW_TILES], func=IDENT)

        v_codes = [
            keep.tile([P, S], U32, name="v_codes0", align_bytes=64),
            keep.tile([P, S], U32, name="v_codes1", tag=f"down_raw{len(DOWN_LOADS) - 1}", align_bytes=64),
        ]
        v_scales = [keep.tile([P, S], U8, name=f"v_scales{a}", align_bytes=64) for a in range(PASSES)]

        def gather_words(a, cols):
            nc.vector.tensor_copy(v_codes[a][:, cols], tab_words[a][:].bitcast(U32).indirect(picks[:, list_columns(cols)]))

        gather_words(0, slice(0, S))
        for a in range(PASSES):
            nc.vector.tensor_copy(v_scales[a][:], tab_scales[:, a, :].indirect(picks[:]))

        h_banks = [psum.tile([P, PACK, HALF], F32, name=f"h_bank{u}", tag=f"bank{u}") for u in range(2)]

        def group_down(a):
            grouped = keep.tile([P, PACK, P, PACK], BF16, name=f"down_grouped{a}", tag="grouped", align_bytes=64)
            for raw, (of_pass, lo, hi) in zip(down_raw, DOWN_LOADS):
                if of_pass == a:
                    source = raw[:].rearrange("p i (m t) -> p m i t", t=PACK)
                    target = grouped[:, :, :, lo:hi].rearrange("p t m i -> p m i t")
                    nc.scalar.copy(out=target[:, VECTOR_PLACES:], in_=source[:, VECTOR_PLACES:])
                    nc.vector.tensor_copy(out=target[:, :VECTOR_PLACES], in_=source[:, :VECTOR_PLACES])
            return grouped

        def quantize_down(a, grouped, slices):
            codes = keep.tile([P, PACK, P], U32, name=f"down_codes{a}", align_bytes=64)
            scales = keep.tile([P, PACK, P], U8, name=f"down_scales{a}", align_bytes=64)
            for t in range(0, PACK, slices):
                nc.vector.quantize_mx(
                    out=codes[:, t : t + slices, :].rearrange("p t m -> p (t m)").bitcast(FP8X4),
                    scales=scales[:, t : t + slices, :].rearrange("p t m -> p (t m)"),
                    in_=grouped[:, t : t + slices].rearrange("p t m i -> p (t m i)"),
                )
            return codes, scales

        def h_passes(a, u, down_q):
            cols = half_columns(u)
            for t in range(PACK):
                nc.tensor.matmul_mx(
                    out=h_banks[u][:, t, :],
                    lhsT=down_q[0][:, t, :].bitcast(FP8X4),
                    lhsT_scale=down_q[1][:, t, :],
                    rhs=v_codes[a][:, cols].bitcast(FP8X4),
                    rhs_scale=v_scales[a][:, cols],
                    start=(a == 0 and t == 0),
                    stop=(a == PASSES - 1 and t == PACK - 1),
                )

        down_q = quantize_down(0, group_down(0), PACK)
        for u in range(2):
            h_passes(0, u, down_q)
        last_grouped = group_down(1)
        gather_words(1, half_columns(0))
        down_q = quantize_down(1, last_grouped, PACK // 2)
        gather_words(1, half_columns(1))
        for u in range(2):
            h_passes(1, u, down_q)

        def group_up(copy, i, grouped):
            u = [lo <= i < hi for lo, hi in UP_LOADS].index(True)
            first = (i - UP_LOADS[u][0]) * P
            source = up_raw[u][:, :, first : first + P].rearrange("p e (c n) -> p c e n", n=LINE)
            copy(out=grouped.rearrange("p (c n) e -> p c e n", n=LINE), in_=source)

        def quantize_up(i, grouped):
            codes = keep.tile([P, P], U32, name=f"up_codes{i}", tag=f"up{i}", align_bytes=64)
            scales = keep.tile([P, P], U8, name=f"up_scales{i}", align_bytes=64)
            nc.vector.quantize_mx(out=codes[:].bitcast(FP8X4), scales=scales[:], in_=grouped.rearrange("p n e -> p (n e)"))
            return codes, scales

        h_codes = keep.tile([P, S], U32, name="h_codes", align_bytes=64)
        h_scales = keep.tile([P, S], U8, name="h_scales", align_bytes=64)

        def quantize_h(u):
            grouped = keep.tile([P, HALF, PACK], BF16, name=f"h_grouped{u}", align_bytes=64)
            nc.scalar.copy(out=grouped[:], in_=h_banks[u][:].rearrange("p t j -> p j t"))
            cols = half_columns(u)
            nc.vector.quantize_mx(
                out=h_codes[:, cols].bitcast(FP8X4), scales=h_scales[:, cols], in_=grouped[:].rearrange("p j t -> p (j t)")
            )

        def open_sum(i, bank, halves):
            u = [lo <= i < hi for lo, hi in W4_LOADS].index(True)
            first = (i - W4_LOADS[u][0]) * 2 * P
            for a in range(PASSES):
                for h in halves:
                    cols = half_columns(h)
                    nc.tensor.matmul_mx(
                        out=bank[:, cols],
                        lhsT=w4_codes[u][:, a, first : first + 2 * P].bitcast(FP4X4),
                        lhsT_scale=w4_scale[:, a, i * P : (i + 1) * P],
                        rhs=v_codes[a][:, cols].bitcast(FP8X4),
                        rhs_scale=v_scales[a][:, cols],
                        start=(a == 0 and h == halves[0]),
                        stop=False,
                    )

        def close_and_scatter(i, bank, halves, up_tile, y):
            cols = slice(halves[0] * HALF, (halves[-1] + 1) * HALF)
            nc.tensor.matmul_mx(
                out=bank[:, cols],
                lhsT=up_tile[0][:].bitcast(FP8X4),
                lhsT_scale=up_tile[1][:],
                rhs=h_codes[:, cols].bitcast(FP8X4),
                rhs_scale=h_scales[:, cols],
                start=False,
                stop=True,
            )
            nc.scalar.activation(out=y[:, cols], in_=bank[:, cols], func=IDENT, bias=bias[:, i : i + 1])
            page = pages[i % PAGES]
            nc.vector.tensor_tensor(page[:].indirect(places[:, list_columns(cols)]), y[:, cols], weights[:, cols], MULT)

        first_grouped = keep.tile([P, FIRST_UP_TILES, P, PACK], BF16, name="first_grouped", tag="grouped", align_bytes=64)
        for i in range(FIRST_UP_TILES):
            group_up(nc.vector.tensor_copy, i, first_grouped[:, i])
        up_q = {0: quantize_up(0, first_grouped[:, 0])}
        quantize_h(0)
        up_q[1] = quantize_up(1, first_grouped[:, 1])
        quantize_h(1)

        for i in range(ROW_TILES):
            y = keep.tile([P, S], F32, name=f"y{i}", tag=f"y{i % Y_TILES}", align_bytes=64)
            if FIRST_UP_TILES <= i + 1 < ROW_TILES:
                next_grouped = keep.tile([P, P, PACK], BF16, name=f"up_grouped{i + 1}", tag=f"up{i - 1}", align_bytes=64)
                group_up(nc.scalar.copy, i + 1, next_grouped[:])
                up_q[i + 1] = quantize_up(i + 1, next_grouped[:])
            for halves in ((0,), (1,)) if i == 0 else ((0, 1),):
                bank = psum.tile([P, S], F32, name=f"y_bank{i}_{halves[0]}", tag=f"bank{(i + halves[-1]) % 2}")
                open_sum(i, bank, halves)
                close_and_scatter(i, bank, halves, up_q[i], y)
            nc.sync.dma_start(out=out[i * P : (i + 1) * P, :], in_=pages[i % PAGES][:])
